import numpy as np, ml_dtypes
CORES = [113,118,241,246]
N = 4
import mx_ref
NC, G = 128, 2
C = np.float32(0.019)
BF = ml_dtypes.bfloat16
def cut(t, i, w=512):
    return t[:, w * i:w * i + w]
def tile(rs):
    return np.stack(rs, axis=2).reshape(128, -1).astype(BF)
def layer(w, X):
    out = []
    for i in range(G):
        for t in range(len(X)):
            p = mx_ref.matmul(mx_ref.quantize(cut(w, len(X) * i + t)), X[t])
            z = p if t == 0 else z + p
        out.append(z)
    return out
def act(Z):
    return [np.maximum(s * z, 0) * C for z in Z for s in (1, -1)]
def pick(b):
    s = np.zeros((128, 128, 4), np.float32)
    s[np.arange(128), np.arange(128), b] = 1.0
    return mx_ref.quantize(s.reshape(128, 512).astype(BF))
def setup_inputs(rng):
    def f(*shape):
        return mx_ref.flush((rng.standard_normal(shape, dtype=np.float32) * np.exp2(rng.integers(-2, 3, shape[:-1] + (1,)))).astype(BF))
    return {"a": f(N, 128, G * 512), "b": f(N, 128, N * 4 * NC)}
def setup_inputs_blocks(rng):
    d = setup_inputs(rng)
    for k in ("a", "b"): d[k] = mx_ref.spread(d[k], rng, 4)
    return d
def setup_inputs_wide(rng):
    d = setup_inputs(rng)
    for k in ("a", "b"): d[k] = mx_ref.flush((d[k].astype(np.float32) * np.exp2(rng.integers(-8, 9, (N, 1, 1))).astype(np.float32)).astype(BF))
    return d
def reference(a, b):
    S = [pick(t) for t in range(4)]
    y = np.zeros((N, 128, NC, 4), np.float32)
    for c in range(N):
        for r in range(N):
            q = mx_ref.quantize(tile(act(layer(a[r], [mx_ref.quantize(cut(b[r], c, 4 * NC))]))))
            p = np.stack([mx_ref.matmul(S[t], q) for t in range(4)], axis=2)
            y[c] = p if r == 0 else y[c] + p
    return {"y": y.reshape(N, 128, 4 * NC)}

@@ -1,0 +1,209 @@
+from concourse.bass import DstId, RemoteDMATransfer
+from concourse.mybir import dt, AluOpType, ActivationFunctionType
+
+N = 4
+NC = 128
+TW = 4 * NC
+C = 0.019
+BANK = 512
+
+PLAN = (("c", (0,)), ("s", (0,)), ("c", (1, 2)), ("s", (1, 2)))
+
+SCRATCH = {
+    "a_t": ("sbuf", [128, 2 * TW], "bfloat16"),
+    "b_t": ("sbuf", [128, N * TW], "bfloat16"),
+    "a_q": ("sbuf", [128, 2 * NC], "float8_e4m3fn_x4"),
+    "a_s": ("sbuf", [128, 2 * NC], "uint8"),
+    "b_q": ("sbuf", [128, N * NC], "float8_e4m3fn_x4"),
+    "b_s": ("sbuf", [128, N * NC], "uint8"),
+    "e_t": ("sbuf", [128, TW + 8], "bfloat16"),
+    "s_q": ("sbuf", [128, 4 * NC], "float8_e4m3fn_x4"),
+    "s_s": ("sbuf", [128, 4 * NC], "uint8"),
+    "g_t": ("sbuf", [128, N * TW], "bfloat16"),
+    "g_q": ("sbuf", [128, N * NC], "float8_e4m3fn_x4"),
+    "g_s": ("sbuf", [128, N * NC], "uint8"),
+    "l_q": ("sbuf", [128, (N - 1) * NC], "float8_e4m3fn_x4"),
+    "l_s": ("sbuf", [128, (N - 1) * NC], "uint8"),
+    "y_t": ("sbuf", [128, TW], "float32"),
+    "ps": ("psum", [128, 8 * BANK], "float32"),
+}
+
+SEMAPHORES = (["ld_a", "e_fill", "e_sel", "q_s", "q_a", "copied", "stored", "sent"]
+              + ["%s%d" % (n, k) for n in ("ld_b", "q_b", "z0_", "z1_", "act_s", "act_v", "q_g", "y_") for k in range(4)]
+              + ["arr%d" % k for k in range(N - 1)])
+
+
+def _engines(mask):
+    return [i for i in range(mask.bit_length()) if (mask >> i) & 1]
+
+
+def _as_mask(engines):
+    m = 0
+    for i in engines:
+        m |= 1 << i
+    return m
+
+
+def _on_chip(a, b, topo):
+    return topo.host(a) == topo.host(b) and topo.chip(a) == topo.chip(b)
+
+
+def _peers(core, cores, topo):
+    return sorted([c for c in cores if c != core], key=lambda c: (_on_chip(c, core, topo), topo.die(c) == topo.die(core)))
+
+
+def _calls(core, cores, topo):
+    peers = _peers(core, cores, topo)
+    away = 0
+    for c in peers:
+        if not _on_chip(c, core, topo):
+            away |= topo.mask(core, c)
+    calls = []
+    for kind, group in PLAN:
+        dsts = [peers[i] for i in group]
+        far = [c for c in dsts if not _on_chip(c, core, topo)]
+        parts = []
+        for c in dsts:
+            if c in far:
+                e = _engines(topo.mask(core, c))
+                n = len(e) // len(far)
+                i = far.index(c)
+                parts.append((c, _as_mask(e[n * i:n * i + n])))
+            else:
+                parts.append((c, topo.mask(core, c) & ~away))
+        calls.append((kind, parts))
+    return calls
+
+
+def _slot(sender, receiver, cores):
+    return [c for c in cores if c != receiver].index(sender)
+
+
+def rank_program(g, core, T, topo):
+    rank = T.rank_of(core)
+    if rank is None:
+        return
+    cores = list(T.cores)
+    sem = T.sem
+    peers = _peers(core, cores, topo)
+    order = [T.rank_of(c) for c in peers] + [rank]
+
+    def cols(c, w):
+        return slice(w * c, w * c + w)
+
+    def bank(k):
+        return T.ps[:, BANK * k:BANK * k + NC]
+
+    g.sync.dma_start(T.a_t[:], T.a[:]).then_inc(sem.ld_a, 16)
+    for k, c in enumerate(order):
+        q = g.scalar if k % 2 == 0 else g.sync
+        q.dma_start(T.b_t[:, cols(c, TW)], T.b[:, cols(c, TW)]).then_inc(sem["ld_b%d" % k], 16)
+
+    e_all = T.e_t[:, 0:TW + 3]
+    g.vector.memset(e_all, 1.0).then_inc(sem.e_fill, 1)
+    g.wait_ge(sem.e_fill, 1)
+    g.affine_select(e_all, e_all, [[-1, TW + 3]], AluOpType.is_equal, 0.0, 3, 4).then_inc(sem.e_sel, 1)
+    g.vector.wait_ge(sem.e_sel, 1)
+    for b in range(4):
+        g.vector.quantize_mx(T.s_q[:, cols(b, NC)], T.s_s[:, cols(b, NC)], T.e_t[:, 3 - b:3 - b + TW]).then_inc(sem.q_s, 1)
+
+    def quant_b(k):
+        c = order[k]
+        g.vector.wait_ge(sem["ld_b%d" % k], 16)
+        g.vector.quantize_mx(T.b_q[:, cols(c, NC)], T.b_s[:, cols(c, NC)], T.b_t[:, cols(c, TW)]).then_inc(sem["q_b%d" % k], 1)
+
+    def signs_v(k):
+        c = order[k]
+        g.vector.wait_ge(sem["z1_%d" % k], 1)
+        g.vector.tensor_scalar(T.g_t[:, TW * c + 2:TW * c + TW:4], bank(2 * k + 1), C, 0.0,
+                               AluOpType.mult, AluOpType.max).then_inc(sem["act_v%d" % k], 1)
+        g.vector.tensor_scalar(T.g_t[:, TW * c + 3:TW * c + TW:4], bank(2 * k + 1), -C, 0.0,
+                               AluOpType.mult, AluOpType.max).then_inc(sem["act_v%d" % k], 1)
+
+    def quant_g(k):
+        c = order[k]
+        g.vector.wait_ge(sem["act_v%d" % k], 2)
+        g.vector.wait_ge(sem["act_s%d" % k], 2)
+        g.vector.quantize_mx(T.g_q[:, cols(c, NC)], T.g_s[:, cols(c, NC)], T.g_t[:, cols(c, TW)]).then_inc(sem["q_g%d" % k], 1)
+
+    g.vector.wait_ge(sem.ld_a, 16)
+    g.vector.quantize_mx(T.a_q[:], T.a_s[:], T.a_t[:]).then_inc(sem.q_a, 1)
+    quant_b(0); signs_v(0); quant_g(0)
+    quant_b(1); quant_b(2); signs_v(1); quant_g(1)
+    quant_b(3); signs_v(2); quant_g(2)
+    signs_v(3); quant_g(3)
+
+    for k, c in enumerate(order):
+        g.scalar.wait_ge(sem["z0_%d" % k], 1)
+        g.scalar.activation(T.g_t[:, TW * c + 0:TW * c + TW:4], bank(2 * k), ActivationFunctionType.Relu,
+                            scale=C).then_inc(sem["act_s%d" % k], 1)
+        g.scalar.activation(T.g_t[:, TW * c + 1:TW * c + TW:4], bank(2 * k), ActivationFunctionType.Relu,
+                            scale=-C).then_inc(sem["act_s%d" % k], 1)
+
+    g.tensor.wait_ge(sem.q_a, 1)
+    for k, c in enumerate(order):
+        g.tensor.wait_ge(sem["q_b%d" % k], 1)
+        for i in range(2):
+            g.tensor.matmul_mx(bank(2 * k + i), T.a_q[:, cols(i, NC)], T.a_s[:, cols(i, NC)],
+                               T.b_q[:, cols(c, NC)], T.b_s[:, cols(c, NC)], True, True).then_inc(sem["z%d_%d" % (i, k)], 1)
+
+    sent = 0
+    for kind, parts in _calls(core, cores, topo):
+        transfers = []
+        for d, mask in parts:
+            g.wait_ge(sem["q_g%d" % peers.index(d)], 1)
+            c, s = T.rank_of(d), _slot(core, d, cores)
+            if kind == "c":
+                src, dst = T.g_q[:, cols(c, NC)].bitcast(dt.uint8), T.l_q[:, cols(s, NC)].bitcast(dt.uint8)
+            else:
+                src, dst = T.g_s[:, cols(c, NC)], T.l_s[:, cols(s, NC)]
+            rid, pid = topo.addr(d, core)
+            transfers.append((src, dst, rid, pid, mask, sem["arr%d" % s]))
+            sent += len(_engines(mask))
+        if len(transfers) == 1:
+            src, dst, rid, pid, mask, rs = transfers[0]
+            g.remote_dma(dst, src, rs, sem.sent, pid, rid, mask)
+        else:
+            g.remote_dma_fused([RemoteDMATransfer(dst_ids=[DstId(rid=rid, pnc=pid)], dma_engine_mask=mask, remote_sem=rs,
+                                                  src=src, dst=dst) for src, dst, rid, pid, mask, rs in transfers],
+                               local_sem=sem.sent)
+
+    g.tensor.wait_ge(sem.q_s, 4)
+    g.tensor.wait_ge(sem.q_g3, 1)
+    for k in range(2):
+        g.tensor.wait_ge(sem["act_s%d" % k], 2)
+        g.tensor.wait_ge(sem["act_v%d" % k], 2)
+    for b in range(4):
+        g.tensor.matmul_mx(bank(b), T.s_q[:, cols(b, NC)], T.s_s[:, cols(b, NC)],
+                           T.g_q[:, cols(rank, NC)], T.g_s[:, cols(rank, NC)], True, False)
+    due = []
+    for s in cores:
+        if s == core:
+            continue
+        last, count = 0, 0
+        for i, (kind, parts) in enumerate(_calls(s, cores, topo)):
+            for d, mask in parts:
+                if d == core:
+                    last, count = i, count + len(_engines(mask))
+        due.append((last, not _on_chip(s, core, topo), s, count))
+    due.sort()
+    for j, (last, off, s, count) in enumerate(due):
+        slot = _slot(s, core, cores)
+        g.tensor.wait_ge(sem["arr%d" % slot], count)
+        for b in range(4):
+            mm = g.tensor.matmul_mx(bank(b), T.s_q[:, cols(b, NC)], T.s_s[:, cols(b, NC)],
+                                    T.l_q[:, cols(slot, NC)], T.l_s[:, cols(slot, NC)], False, j == len(due) - 1)
+            if j == len(due) - 1:
+                mm.then_inc(sem["y_%d" % b], 1)
+
+    for b in range(4):
+        if b % 2 == 0:
+            g.scalar.wait_ge(sem["y_%d" % b], 1)
+            g.scalar.activation(T.y_t[:, b:TW:4], bank(b), ActivationFunctionType.Copy).then_inc(sem.copied, 1)
+        else:
+            g.vector.wait_ge(sem["y_%d" % b], 1)
+            g.vector.tensor_copy(T.y_t[:, b:TW:4], bank(b)).then_inc(sem.copied, 1)
+    g.sync.wait_ge(sem.copied, 4)
+    g.sync.dma_start(T.y[:], T.y_t[:]).then_inc(sem.stored, 16)
+    g.sync.wait_ge(sem.stored, 16)
+    g.wait_ge(sem.sent, sent)

@@ -1,4 +1,3 @@
-from concourse.bass import DstId, RemoteDMATransfer
 from concourse.mybir import dt, AluOpType, ActivationFunctionType
 
 N = 4
@@ -7,8 +6,6 @@ TW = 4 * NC
 C = 0.019
 BANK = 512
 
-PLAN = (("c", (0,)), ("s", (0,)), ("c", (1, 2)), ("s", (1, 2)))
-
 SCRATCH = {
     "a_t": ("sbuf", [128, 2 * TW], "bfloat16"),
     "b_t": ("sbuf", [128, N * TW], "bfloat16"),
@@ -16,6 +13,7 @@ SCRATCH = {
     "a_s": ("sbuf", [128, 2 * NC], "uint8"),
     "b_q": ("sbuf", [128, N * NC], "float8_e4m3fn_x4"),
     "b_s": ("sbuf", [128, N * NC], "uint8"),
+    "i_t": ("sbuf", [128, NC], "bfloat16"),
     "e_t": ("sbuf", [128, TW + 8], "bfloat16"),
     "s_q": ("sbuf", [128, 4 * NC], "float8_e4m3fn_x4"),
     "s_s": ("sbuf", [128, 4 * NC], "uint8"),
@@ -28,20 +26,13 @@ SCRATCH = {
     "ps": ("psum", [128, 8 * BANK], "float32"),
 }
 
-SEMAPHORES = (["ld_a", "e_fill", "e_sel", "q_s", "q_a", "copied", "stored", "sent"]
+SEMAPHORES = (["ld_a", "e_fill", "e_zero", "e_sel", "e_done", "q_s", "s_arr", "q_a0", "q_a1", "copied", "stored", "sent"]
               + ["%s%d" % (n, k) for n in ("ld_b", "q_b", "z0_", "z1_", "act_s", "act_v", "q_g", "y_") for k in range(4)]
               + ["arr%d" % k for k in range(N - 1)])
 
 
-def _engines(mask):
-    return [i for i in range(mask.bit_length()) if (mask >> i) & 1]
-
-
-def _as_mask(engines):
-    m = 0
-    for i in engines:
-        m |= 1 << i
-    return m
+def _count(mask):
+    return sum((mask >> i) & 1 for i in range(mask.bit_length()))
 
 
 def _on_chip(a, b, topo):
@@ -52,27 +43,9 @@ def _peers(core, cores, topo):
     return sorted([c for c in cores if c != core], key=lambda c: (_on_chip(c, core, topo), topo.die(c) == topo.die(core)))
 
 
-def _calls(core, cores, topo):
-    peers = _peers(core, cores, topo)
-    away = 0
-    for c in peers:
-        if not _on_chip(c, core, topo):
-            away |= topo.mask(core, c)
-    calls = []
-    for kind, group in PLAN:
-        dsts = [peers[i] for i in group]
-        far = [c for c in dsts if not _on_chip(c, core, topo)]
-        parts = []
-        for c in dsts:
-            if c in far:
-                e = _engines(topo.mask(core, c))
-                n = len(e) // len(far)
-                i = far.index(c)
-                parts.append((c, _as_mask(e[n * i:n * i + n])))
-            else:
-                parts.append((c, topo.mask(core, c) & ~away))
-        calls.append((kind, parts))
-    return calls
+def _home(core, cores, topo):
+    home = sorted(c for c in cores if _on_chip(c, core, topo))
+    return home if 4 % len(home) == 0 else [core]
 
 
 def _slot(sender, receiver, cores):
@@ -87,9 +60,12 @@ def rank_program(g, core, T, topo):
     sem = T.sem
     peers = _peers(core, cores, topo)
     order = [T.rank_of(c) for c in peers] + [rank]
+    home = _home(core, cores, topo)
+    share = 4 // len(home)
+    first = share * home.index(core)
 
-    def cols(c, w):
-        return slice(w * c, w * c + w)
+    def cols(c, w, n=1):
+        return slice(w * c, w * c + w * n)
 
     def bank(k):
         return T.ps[:, BANK * k:BANK * k + NC]
@@ -99,39 +75,60 @@ def rank_program(g, core, T, topo):
         q = g.scalar if k % 2 == 0 else g.sync
         q.dma_start(T.b_t[:, cols(c, TW)], T.b[:, cols(c, TW)]).then_inc(sem["ld_b%d" % k], 16)
 
-    e_all = T.e_t[:, 0:TW + 3]
-    g.vector.memset(e_all, 1.0).then_inc(sem.e_fill, 1)
+    g.vector.memset(T.i_t[:], 1.0).then_inc(sem.e_fill, 1)
+    g.vector.memset(T.e_t[:, 0:TW + 3], 0.0).then_inc(sem.e_zero, 1)
     g.wait_ge(sem.e_fill, 1)
-    g.affine_select(e_all, e_all, [[-1, TW + 3]], AluOpType.is_equal, 0.0, 3, 4).then_inc(sem.e_sel, 1)
+    g.affine_select(T.i_t[:], T.i_t[:], [[-1, NC]], AluOpType.is_equal, 0.0, 0, 1).then_inc(sem.e_sel, 1)
     g.vector.wait_ge(sem.e_sel, 1)
-    for b in range(4):
+    g.vector.wait_ge(sem.e_zero, 1)
+    g.vector.tensor_copy(T.e_t[:, 3:TW + 3:4], T.i_t[:]).then_inc(sem.e_done, 1)
+    g.vector.wait_ge(sem.e_done, 1)
+    for b in range(first, first + share):
         g.vector.quantize_mx(T.s_q[:, cols(b, NC)], T.s_s[:, cols(b, NC)], T.e_t[:, 3 - b:3 - b + TW]).then_inc(sem.q_s, 1)
+
+    sent = 0
+    s_due = 0
+    g.wait_ge(sem.q_s, share)
+    for d in home:
+        if d == core:
+            continue
+        rid, pid = topo.addr(d, core)
+        mask = topo.mask(core, d)
+        part = cols(first, NC, share)
+        g.remote_dma(T.s_q[:, part].bitcast(dt.uint8), T.s_q[:, part].bitcast(dt.uint8), sem.s_arr, sem.sent, pid, rid, mask)
+        g.remote_dma(T.s_s[:, part], T.s_s[:, part], sem.s_arr, sem.sent, pid, rid, mask)
+        sent += 2 * _count(mask)
+        s_due += 2 * _count(topo.mask(d, core))
+
+    def quant_a(i):
+        g.vector.quantize_mx(T.a_q[:, cols(i, NC)], T.a_s[:, cols(i, NC)], T.a_t[:, cols(i, TW)]).then_inc(sem["q_a%d" % i], 1)
 
     def quant_b(k):
         c = order[k]
         g.vector.wait_ge(sem["ld_b%d" % k], 16)
         g.vector.quantize_mx(T.b_q[:, cols(c, NC)], T.b_s[:, cols(c, NC)], T.b_t[:, cols(c, TW)]).then_inc(sem["q_b%d" % k], 1)
 
-    def signs_v(k):
+    def sign_v(k):
         c = order[k]
         g.vector.wait_ge(sem["z1_%d" % k], 1)
         g.vector.tensor_scalar(T.g_t[:, TW * c + 2:TW * c + TW:4], bank(2 * k + 1), C, 0.0,
                                AluOpType.mult, AluOpType.max).then_inc(sem["act_v%d" % k], 1)
-        g.vector.tensor_scalar(T.g_t[:, TW * c + 3:TW * c + TW:4], bank(2 * k + 1), -C, 0.0,
-                               AluOpType.mult, AluOpType.max).then_inc(sem["act_v%d" % k], 1)
 
     def quant_g(k):
         c = order[k]
-        g.vector.wait_ge(sem["act_v%d" % k], 2)
-        g.vector.wait_ge(sem["act_s%d" % k], 2)
+        g.vector.wait_ge(sem["act_v%d" % k], 1)
+        g.vector.wait_ge(sem["act_s%d" % k], 3)
         g.vector.quantize_mx(T.g_q[:, cols(c, NC)], T.g_s[:, cols(c, NC)], T.g_t[:, cols(c, TW)]).then_inc(sem["q_g%d" % k], 1)
 
     g.vector.wait_ge(sem.ld_a, 16)
-    g.vector.quantize_mx(T.a_q[:], T.a_s[:], T.a_t[:]).then_inc(sem.q_a, 1)
-    quant_b(0); signs_v(0); quant_g(0)
-    quant_b(1); quant_b(2); signs_v(1); quant_g(1)
-    quant_b(3); signs_v(2); quant_g(2)
-    signs_v(3); quant_g(3)
+    quant_a(0)
+    quant_b(0)
+    quant_a(1)
+    for k in range(N):
+        sign_v(k)
+        if k + 1 < N:
+            quant_b(k + 1)
+        quant_g(k)
 
     for k, c in enumerate(order):
         g.scalar.wait_ge(sem["z0_%d" % k], 1)
@@ -139,57 +136,45 @@ def rank_program(g, core, T, topo):
                             scale=C).then_inc(sem["act_s%d" % k], 1)
         g.scalar.activation(T.g_t[:, TW * c + 1:TW * c + TW:4], bank(2 * k), ActivationFunctionType.Relu,
                             scale=-C).then_inc(sem["act_s%d" % k], 1)
+        g.scalar.wait_ge(sem["act_v%d" % k], 1)
+        g.scalar.activation(T.g_t[:, TW * c + 3:TW * c + TW:4], bank(2 * k + 1), ActivationFunctionType.Relu,
+                            scale=-C).then_inc(sem["act_s%d" % k], 1)
 
-    g.tensor.wait_ge(sem.q_a, 1)
     for k, c in enumerate(order):
         g.tensor.wait_ge(sem["q_b%d" % k], 1)
         for i in range(2):
+            if k == 0:
+                g.tensor.wait_ge(sem["q_a%d" % i], 1)
             g.tensor.matmul_mx(bank(2 * k + i), T.a_q[:, cols(i, NC)], T.a_s[:, cols(i, NC)],
                                T.b_q[:, cols(c, NC)], T.b_s[:, cols(c, NC)], True, True).then_inc(sem["z%d_%d" % (i, k)], 1)
 
-    sent = 0
-    for kind, parts in _calls(core, cores, topo):
-        transfers = []
-        for d, mask in parts:
-            g.wait_ge(sem["q_g%d" % peers.index(d)], 1)
-            c, s = T.rank_of(d), _slot(core, d, cores)
-            if kind == "c":
-                src, dst = T.g_q[:, cols(c, NC)].bitcast(dt.uint8), T.l_q[:, cols(s, NC)].bitcast(dt.uint8)
-            else:
-                src, dst = T.g_s[:, cols(c, NC)], T.l_s[:, cols(s, NC)]
-            rid, pid = topo.addr(d, core)
-            transfers.append((src, dst, rid, pid, mask, sem["arr%d" % s]))
-            sent += len(_engines(mask))
-        if len(transfers) == 1:
-            src, dst, rid, pid, mask, rs = transfers[0]
-            g.remote_dma(dst, src, rs, sem.sent, pid, rid, mask)
-        else:
-            g.remote_dma_fused([RemoteDMATransfer(dst_ids=[DstId(rid=rid, pnc=pid)], dma_engine_mask=mask, remote_sem=rs,
-                                                  src=src, dst=dst) for src, dst, rid, pid, mask, rs in transfers],
-                               local_sem=sem.sent)
+    for k, d in enumerate(peers):
+        c, s = T.rank_of(d), _slot(core, d, cores)
+        rid, pid = topo.addr(d, core)
+        mask = topo.mask(core, d)
+        g.wait_ge(sem["q_g%d" % k], 1)
+        g.remote_dma(T.l_q[:, cols(s, NC)].bitcast(dt.uint8), T.g_q[:, cols(c, NC)].bitcast(dt.uint8),
+                     sem["arr%d" % s], sem.sent, pid, rid, mask)
+        g.remote_dma(T.l_s[:, cols(s, NC)], T.g_s[:, cols(c, NC)], sem["arr%d" % s], sem.sent, pid, rid, mask)
+        sent += 2 * _count(mask)
 
-    g.tensor.wait_ge(sem.q_s, 4)
+    g.tensor.wait_ge(sem.q_s, share)
+    if s_due:
+        g.tensor.wait_ge(sem.s_arr, s_due)
     g.tensor.wait_ge(sem.q_g3, 1)
     for k in range(2):
-        g.tensor.wait_ge(sem["act_s%d" % k], 2)
-        g.tensor.wait_ge(sem["act_v%d" % k], 2)
+        g.tensor.wait_ge(sem["act_s%d" % k], 3)
+        g.tensor.wait_ge(sem["act_v%d" % k], 1)
     for b in range(4):
         g.tensor.matmul_mx(bank(b), T.s_q[:, cols(b, NC)], T.s_s[:, cols(b, NC)],
                            T.g_q[:, cols(rank, NC)], T.g_s[:, cols(rank, NC)], True, False)
-    due = []
-    for s in cores:
-        if s == core:
-            continue
-        last, count = 0, 0
-        for i, (kind, parts) in enumerate(_calls(s, cores, topo)):
-            for d, mask in parts:
-                if d == core:
-                    last, count = i, count + len(_engines(mask))
-        due.append((last, not _on_chip(s, core, topo), s, count))
-    due.sort()
-    for j, (last, off, s, count) in enumerate(due):
+    far = sorted([s for s in cores if s != core and not _on_chip(s, core, topo)],
+                 key=lambda s: _peers(s, cores, topo).index(core))
+    near = [s for s in cores if s != core and _on_chip(s, core, topo)]
+    due = far[:-1] + near + far[-1:]
+    for j, s in enumerate(due):
         slot = _slot(s, core, cores)
-        g.tensor.wait_ge(sem["arr%d" % slot], count)
+        g.tensor.wait_ge(sem["arr%d" % slot], 2 * _count(topo.mask(s, core)))
         for b in range(4):
             mm = g.tensor.matmul_mx(bank(b), T.s_q[:, cols(b, NC)], T.s_s[:, cols(b, NC)],
                                     T.l_q[:, cols(slot, NC)], T.l_s[:, cols(slot, NC)], False, j == len(due) - 1)

@@ -26,7 +26,8 @@ SCRATCH = {
     "ps": ("psum", [128, 8 * BANK], "float32"),
 }
 
-SEMAPHORES = (["ld_a", "e_fill", "e_zero", "e_sel", "e_done", "q_s", "s_arr", "q_a0", "q_a1", "copied", "stored", "sent"]
+SEMAPHORES = (["ld_a0", "ld_a1", "e_fill", "e_zero", "e_sel", "e_done", "q_s0", "q_s", "s_arr", "q_a0", "q_a1", "copied",
+               "stored", "sent"]
               + ["%s%d" % (n, k) for n in ("ld_b", "q_b", "z0_", "z1_", "act_s", "act_v", "q_g", "y_") for k in range(4)]
               + ["arr%d" % k for k in range(N - 1)])
 
@@ -45,7 +46,7 @@ def _peers(core, cores, topo):
 
 def _home(core, cores, topo):
     home = sorted(c for c in cores if _on_chip(c, core, topo))
-    return home if 4 % len(home) == 0 else [core]
+    return home if len(home) <= 4 else [core]
 
 
 def _slot(sender, receiver, cores):
@@ -61,8 +62,11 @@ def rank_program(g, core, T, topo):
     peers = _peers(core, cores, topo)
     order = [T.rank_of(c) for c in peers] + [rank]
     home = _home(core, cores, topo)
-    share = 4 // len(home)
-    first = share * home.index(core)
+    give = home.index(core)
+    mine = [give] + list(range(len(home), 4))
+    slices = mine + [b for b in range(4) if b not in mine]
+    LAST = N - 1
+    by_scalar = [4] * LAST + [2]
 
     def cols(c, w, n=1):
         return slice(w * c, w * c + w * n)
@@ -70,10 +74,21 @@ def rank_program(g, core, T, topo):
     def bank(k):
         return T.ps[:, BANK * k:BANK * k + NC]
 
-    g.sync.dma_start(T.a_t[:], T.a[:]).then_inc(sem.ld_a, 16)
-    for k, c in enumerate(order):
-        q = g.scalar if k % 2 == 0 else g.sync
-        q.dma_start(T.b_t[:, cols(c, TW)], T.b[:, cols(c, TW)]).then_inc(sem["ld_b%d" % k], 16)
+    def load_a(q, i):
+        q.dma_start(T.a_t[:, cols(i, TW)], T.a[:, cols(i, TW)]).then_inc(sem["ld_a%d" % i], 16)
+
+    def load_b(q, k):
+        q.dma_start(T.b_t[:, cols(order[k], TW)], T.b[:, cols(order[k], TW)]).then_inc(sem["ld_b%d" % k], 16)
+
+    load_a(g.sync, 0)
+    load_b(g.scalar, 0)
+    load_a(g.sync, 1)
+    load_b(g.scalar, 1)
+    load_b(g.sync, 2)
+    load_b(g.scalar, 3)
+
+    def quant_s(b, s):
+        g.vector.quantize_mx(T.s_q[:, cols(b, NC)], T.s_s[:, cols(b, NC)], T.e_t[:, 3 - b:3 - b + TW]).then_inc(s, 1)
 
     g.vector.memset(T.i_t[:], 1.0).then_inc(sem.e_fill, 1)
     g.vector.memset(T.e_t[:, 0:TW + 3], 0.0).then_inc(sem.e_zero, 1)
@@ -83,24 +98,25 @@ def rank_program(g, core, T, topo):
     g.vector.wait_ge(sem.e_zero, 1)
     g.vector.tensor_copy(T.e_t[:, 3:TW + 3:4], T.i_t[:]).then_inc(sem.e_done, 1)
     g.vector.wait_ge(sem.e_done, 1)
-    for b in range(first, first + share):
-        g.vector.quantize_mx(T.s_q[:, cols(b, NC)], T.s_s[:, cols(b, NC)], T.e_t[:, 3 - b:3 - b + TW]).then_inc(sem.q_s, 1)
+    quant_s(give, sem.q_s0)
+    later = list(mine[1:])
 
     sent = 0
     s_due = 0
-    g.wait_ge(sem.q_s, share)
+    g.wait_ge(sem.q_s0, 1)
     for d in home:
         if d == core:
             continue
         rid, pid = topo.addr(d, core)
         mask = topo.mask(core, d)
-        part = cols(first, NC, share)
+        part = cols(give, NC)
         g.remote_dma(T.s_q[:, part].bitcast(dt.uint8), T.s_q[:, part].bitcast(dt.uint8), sem.s_arr, sem.sent, pid, rid, mask)
         g.remote_dma(T.s_s[:, part], T.s_s[:, part], sem.s_arr, sem.sent, pid, rid, mask)
         sent += 2 * _count(mask)
         s_due += 2 * _count(topo.mask(d, core))
 
     def quant_a(i):
+        g.vector.wait_ge(sem["ld_a%d" % i], 16)
         g.vector.quantize_mx(T.a_q[:, cols(i, NC)], T.a_s[:, cols(i, NC)], T.a_t[:, cols(i, TW)]).then_inc(sem["q_a%d" % i], 1)
 
     def quant_b(k):
@@ -108,37 +124,39 @@ def rank_program(g, core, T, topo):
         g.vector.wait_ge(sem["ld_b%d" % k], 16)
         g.vector.quantize_mx(T.b_q[:, cols(c, NC)], T.b_s[:, cols(c, NC)], T.b_t[:, cols(c, TW)]).then_inc(sem["q_b%d" % k], 1)
 
-    def sign_v(k):
-        c = order[k]
-        g.vector.wait_ge(sem["z1_%d" % k], 1)
-        g.vector.tensor_scalar(T.g_t[:, TW * c + 2:TW * c + TW:4], bank(2 * k + 1), C, 0.0,
-                               AluOpType.mult, AluOpType.max).then_inc(sem["act_v%d" % k], 1)
-
     def quant_g(k):
         c = order[k]
-        g.vector.wait_ge(sem["act_v%d" % k], 1)
-        g.vector.wait_ge(sem["act_s%d" % k], 3)
+        if by_scalar[k] < 4:
+            g.vector.wait_ge(sem["act_v%d" % k], 4 - by_scalar[k])
+        g.vector.wait_ge(sem["act_s%d" % k], by_scalar[k])
         g.vector.quantize_mx(T.g_q[:, cols(c, NC)], T.g_s[:, cols(c, NC)], T.g_t[:, cols(c, TW)]).then_inc(sem["q_g%d" % k], 1)
 
-    g.vector.wait_ge(sem.ld_a, 16)
     quant_a(0)
     quant_b(0)
     quant_a(1)
-    for k in range(N):
-        sign_v(k)
-        if k + 1 < N:
-            quant_b(k + 1)
+    quant_b(1)
+    for k in range(LAST):
         quant_g(k)
+        if k + 2 < N:
+            quant_b(k + 2)
+            if later:
+                quant_s(later.pop(0), sem.q_s)
+    while later:
+        quant_s(later.pop(0), sem.q_s)
+    c = order[LAST]
+    g.vector.wait_ge(sem["z1_%d" % LAST], 1)
+    g.vector.tensor_scalar(T.g_t[:, TW * c + 2:TW * c + TW:4], bank(2 * LAST + 1), C, 0.0,
+                           AluOpType.mult, AluOpType.max).then_inc(sem["act_v%d" % LAST], 1)
+    g.vector.tensor_scalar(T.g_t[:, TW * c + 3:TW * c + TW:4], bank(2 * LAST + 1), -C, 0.0,
+                           AluOpType.mult, AluOpType.max).then_inc(sem["act_v%d" % LAST], 1)
+    quant_g(LAST)
 
     for k, c in enumerate(order):
-        g.scalar.wait_ge(sem["z0_%d" % k], 1)
-        g.scalar.activation(T.g_t[:, TW * c + 0:TW * c + TW:4], bank(2 * k), ActivationFunctionType.Relu,
-                            scale=C).then_inc(sem["act_s%d" % k], 1)
-        g.scalar.activation(T.g_t[:, TW * c + 1:TW * c + TW:4], bank(2 * k), ActivationFunctionType.Relu,
-                            scale=-C).then_inc(sem["act_s%d" % k], 1)
-        g.scalar.wait_ge(sem["act_v%d" % k], 1)
-        g.scalar.activation(T.g_t[:, TW * c + 3:TW * c + TW:4], bank(2 * k + 1), ActivationFunctionType.Relu,
-                            scale=-C).then_inc(sem["act_s%d" % k], 1)
+        for i in range(by_scalar[k] // 2):
+            g.scalar.wait_ge(sem["z%d_%d" % (i, k)], 1)
+            for j, s in enumerate((C, -C)):
+                g.scalar.activation(T.g_t[:, TW * c + 2 * i + j:TW * c + TW:4], bank(2 * k + i),
+                                    ActivationFunctionType.Relu, scale=s).then_inc(sem["act_s%d" % k], 1)
 
     for k, c in enumerate(order):
         g.tensor.wait_ge(sem["q_b%d" % k], 1)
@@ -158,14 +176,15 @@ def rank_program(g, core, T, topo):
         g.remote_dma(T.l_s[:, cols(s, NC)], T.g_s[:, cols(c, NC)], sem["arr%d" % s], sem.sent, pid, rid, mask)
         sent += 2 * _count(mask)
 
-    g.tensor.wait_ge(sem.q_s, share)
-    if s_due:
-        g.tensor.wait_ge(sem.s_arr, s_due)
-    g.tensor.wait_ge(sem.q_g3, 1)
+    g.tensor.wait_ge(sem.q_s0, 1)
+    if len(mine) > 1:
+        g.tensor.wait_ge(sem.q_s, len(mine) - 1)
+    g.tensor.wait_ge(sem["q_g%d" % LAST], 1)
     for k in range(2):
-        g.tensor.wait_ge(sem["act_s%d" % k], 3)
-        g.tensor.wait_ge(sem["act_v%d" % k], 1)
-    for b in range(4):
+        g.tensor.wait_ge(sem["act_s%d" % k], by_scalar[k])
+    for n, b in enumerate(slices):
+        if n == len(mine) and s_due:
+            g.tensor.wait_ge(sem.s_arr, s_due)
         g.tensor.matmul_mx(bank(b), T.s_q[:, cols(b, NC)], T.s_s[:, cols(b, NC)],
                            T.g_q[:, cols(rank, NC)], T.g_s[:, cols(rank, NC)], True, False)
     far = sorted([s for s in cores if s != core and not _on_chip(s, core, topo)],
@@ -175,14 +194,14 @@ def rank_program(g, core, T, topo):
     for j, s in enumerate(due):
         slot = _slot(s, core, cores)
         g.tensor.wait_ge(sem["arr%d" % slot], 2 * _count(topo.mask(s, core)))
-        for b in range(4):
+        for b in slices:
             mm = g.tensor.matmul_mx(bank(b), T.s_q[:, cols(b, NC)], T.s_s[:, cols(b, NC)],
                                     T.l_q[:, cols(slot, NC)], T.l_s[:, cols(slot, NC)], False, j == len(due) - 1)
             if j == len(due) - 1:
                 mm.then_inc(sem["y_%d" % b], 1)
 
-    for b in range(4):
-        if b % 2 == 0:
+    for n, b in enumerate(slices):
+        if n % 2 == 0:
             g.scalar.wait_ge(sem["y_%d" % b], 1)
             g.scalar.activation(T.y_t[:, b:TW:4], bank(b), ActivationFunctionType.Copy).then_inc(sem.copied, 1)
         else:

from concourse.mybir import dt, AluOpType, ActivationFunctionType

N = 4
NC = 128
TW = 4 * NC
C = 0.019
BANK = 512

SCRATCH = {
    "a_t": ("sbuf", [128, 2 * TW], "bfloat16"),
    "b_t": ("sbuf", [128, N * TW], "bfloat16"),
    "a_q": ("sbuf", [128, 2 * NC], "float8_e4m3fn_x4"),
    "a_s": ("sbuf", [128, 2 * NC], "uint8"),
    "b_q": ("sbuf", [128, N * NC], "float8_e4m3fn_x4"),
    "b_s": ("sbuf", [128, N * NC], "uint8"),
    "i_t": ("sbuf", [128, NC], "bfloat16"),
    "e_t": ("sbuf", [128, TW + 8], "bfloat16"),
    "s_q": ("sbuf", [128, 4 * NC], "float8_e4m3fn_x4"),
    "s_s": ("sbuf", [128, 4 * NC], "uint8"),
    "g_t": ("sbuf", [128, N * TW], "bfloat16"),
    "g_q": ("sbuf", [128, N * NC], "float8_e4m3fn_x4"),
    "g_s": ("sbuf", [128, N * NC], "uint8"),
    "l_q": ("sbuf", [128, (N - 1) * NC], "float8_e4m3fn_x4"),
    "l_s": ("sbuf", [128, (N - 1) * NC], "uint8"),
    "y_t": ("sbuf", [128, TW], "float32"),
    "ps": ("psum", [128, 8 * BANK], "float32"),
}

SEMAPHORES = (["ld_a0", "ld_a1", "e_fill", "e_zero", "e_sel", "e_done", "q_s0", "q_s", "s_arr", "q_a0", "q_a1", "copied",
               "stored", "sent"]
              + ["%s%d" % (n, k) for n in ("ld_b", "q_b", "z0_", "z1_", "act_s", "act_v", "q_g", "y_") for k in range(4)]
              + ["arr%d" % k for k in range(N - 1)])


def _count(mask):
    return sum((mask >> i) & 1 for i in range(mask.bit_length()))


def _on_chip(a, b, topo):
    return topo.host(a) == topo.host(b) and topo.chip(a) == topo.chip(b)


def _peers(core, cores, topo):
    return sorted([c for c in cores if c != core], key=lambda c: (_on_chip(c, core, topo), topo.die(c) == topo.die(core)))


def _home(core, cores, topo):
    home = sorted(c for c in cores if _on_chip(c, core, topo))
    return home if len(home) <= 4 else [core]


def _slot(sender, receiver, cores):
    return [c for c in cores if c != receiver].index(sender)


def rank_program(g, core, T, topo):
    rank = T.rank_of(core)
    if rank is None:
        return
    cores = list(T.cores)
    sem = T.sem
    peers = _peers(core, cores, topo)
    order = [T.rank_of(c) for c in peers] + [rank]
    home = _home(core, cores, topo)
    give = home.index(core)
    mine = [give] + list(range(len(home), 4))
    slices = mine + [b for b in range(4) if b not in mine]
    LAST = N - 1
    by_scalar = [4] * LAST + [2]

    def cols(c, w, n=1):
        return slice(w * c, w * c + w * n)

    def bank(k):
        return T.ps[:, BANK * k:BANK * k + NC]

    def load_a(q, i):
        q.dma_start(T.a_t[:, cols(i, TW)], T.a[:, cols(i, TW)]).then_inc(sem["ld_a%d" % i], 16)

    def load_b(q, k):
        q.dma_start(T.b_t[:, cols(order[k], TW)], T.b[:, cols(order[k], TW)]).then_inc(sem["ld_b%d" % k], 16)

    load_a(g.sync, 0)
    load_b(g.scalar, 0)
    load_a(g.sync, 1)
    load_b(g.scalar, 1)
    load_b(g.sync, 2)
    load_b(g.scalar, 3)

    def quant_s(b, s):
        g.vector.quantize_mx(T.s_q[:, cols(b, NC)], T.s_s[:, cols(b, NC)], T.e_t[:, 3 - b:3 - b + TW]).then_inc(s, 1)

    g.vector.memset(T.i_t[:], 1.0).then_inc(sem.e_fill, 1)
    g.vector.memset(T.e_t[:, 0:TW + 3], 0.0).then_inc(sem.e_zero, 1)
    g.wait_ge(sem.e_fill, 1)
    g.affine_select(T.i_t[:], T.i_t[:], [[-1, NC]], AluOpType.is_equal, 0.0, 0, 1).then_inc(sem.e_sel, 1)
    g.vector.wait_ge(sem.e_sel, 1)
    g.vector.wait_ge(sem.e_zero, 1)
    g.vector.tensor_copy(T.e_t[:, 3:TW + 3:4], T.i_t[:]).then_inc(sem.e_done, 1)
    g.vector.wait_ge(sem.e_done, 1)
    quant_s(give, sem.q_s0)
    later = list(mine[1:])

    sent = 0
    s_due = 0
    g.wait_ge(sem.q_s0, 1)
    for d in home:
        if d == core:
            continue
        rid, pid = topo.addr(d, core)
        mask = topo.mask(core, d)
        part = cols(give, NC)
        g.remote_dma(T.s_q[:, part].bitcast(dt.uint8), T.s_q[:, part].bitcast(dt.uint8), sem.s_arr, sem.sent, pid, rid, mask)
        g.remote_dma(T.s_s[:, part], T.s_s[:, part], sem.s_arr, sem.sent, pid, rid, mask)
        sent += 2 * _count(mask)
        s_due += 2 * _count(topo.mask(d, core))

    def quant_a(i):
        g.vector.wait_ge(sem["ld_a%d" % i], 16)
        g.vector.quantize_mx(T.a_q[:, cols(i, NC)], T.a_s[:, cols(i, NC)], T.a_t[:, cols(i, TW)]).then_inc(sem["q_a%d" % i], 1)

    def quant_b(k):
        c = order[k]
        g.vector.wait_ge(sem["ld_b%d" % k], 16)
        g.vector.quantize_mx(T.b_q[:, cols(c, NC)], T.b_s[:, cols(c, NC)], T.b_t[:, cols(c, TW)]).then_inc(sem["q_b%d" % k], 1)

    def quant_g(k):
        c = order[k]
        if by_scalar[k] < 4:
            g.vector.wait_ge(sem["act_v%d" % k], 4 - by_scalar[k])
        g.vector.wait_ge(sem["act_s%d" % k], by_scalar[k])
        g.vector.quantize_mx(T.g_q[:, cols(c, NC)], T.g_s[:, cols(c, NC)], T.g_t[:, cols(c, TW)]).then_inc(sem["q_g%d" % k], 1)

    quant_a(0)
    quant_b(0)
    quant_a(1)
    quant_b(1)
    for k in range(LAST):
        quant_g(k)
        if k + 2 < N:
            quant_b(k + 2)
            if later:
                quant_s(later.pop(0), sem.q_s)
    while later:
        quant_s(later.pop(0), sem.q_s)
    c = order[LAST]
    g.vector.wait_ge(sem["z1_%d" % LAST], 1)
    g.vector.tensor_scalar(T.g_t[:, TW * c + 2:TW * c + TW:4], bank(2 * LAST + 1), C, 0.0,
                           AluOpType.mult, AluOpType.max).then_inc(sem["act_v%d" % LAST], 1)
    g.vector.tensor_scalar(T.g_t[:, TW * c + 3:TW * c + TW:4], bank(2 * LAST + 1), -C, 0.0,
                           AluOpType.mult, AluOpType.max).then_inc(sem["act_v%d" % LAST], 1)
    quant_g(LAST)

    for k, c in enumerate(order):
        for i in range(by_scalar[k] // 2):
            g.scalar.wait_ge(sem["z%d_%d" % (i, k)], 1)
            for j, s in enumerate((C, -C)):
                g.scalar.activation(T.g_t[:, TW * c + 2 * i + j:TW * c + TW:4], bank(2 * k + i),
                                    ActivationFunctionType.Relu, scale=s).then_inc(sem["act_s%d" % k], 1)

    for k, c in enumerate(order):
        g.tensor.wait_ge(sem["q_b%d" % k], 1)
        for i in range(2):
            if k == 0:
                g.tensor.wait_ge(sem["q_a%d" % i], 1)
            g.tensor.matmul_mx(bank(2 * k + i), T.a_q[:, cols(i, NC)], T.a_s[:, cols(i, NC)],
                               T.b_q[:, cols(c, NC)], T.b_s[:, cols(c, NC)], True, True).then_inc(sem["z%d_%d" % (i, k)], 1)

    for k, d in enumerate(peers):
        c, s = T.rank_of(d), _slot(core, d, cores)
        rid, pid = topo.addr(d, core)
        mask = topo.mask(core, d)
        g.wait_ge(sem["q_g%d" % k], 1)
        g.remote_dma(T.l_q[:, cols(s, NC)].bitcast(dt.uint8), T.g_q[:, cols(c, NC)].bitcast(dt.uint8),
                     sem["arr%d" % s], sem.sent, pid, rid, mask)
        g.remote_dma(T.l_s[:, cols(s, NC)], T.g_s[:, cols(c, NC)], sem["arr%d" % s], sem.sent, pid, rid, mask)
        sent += 2 * _count(mask)

    g.tensor.wait_ge(sem.q_s0, 1)
    if len(mine) > 1:
        g.tensor.wait_ge(sem.q_s, len(mine) - 1)
    g.tensor.wait_ge(sem["q_g%d" % LAST], 1)
    for k in range(2):
        g.tensor.wait_ge(sem["act_s%d" % k], by_scalar[k])
    for n, b in enumerate(slices):
        if n == len(mine) and s_due:
            g.tensor.wait_ge(sem.s_arr, s_due)
        g.tensor.matmul_mx(bank(b), T.s_q[:, cols(b, NC)], T.s_s[:, cols(b, NC)],
                           T.g_q[:, cols(rank, NC)], T.g_s[:, cols(rank, NC)], True, False)
    far = sorted([s for s in cores if s != core and not _on_chip(s, core, topo)],
                 key=lambda s: _peers(s, cores, topo).index(core))
    near = [s for s in cores if s != core and _on_chip(s, core, topo)]
    due = far[:-1] + near + far[-1:]
    for j, s in enumerate(due):
        slot = _slot(s, core, cores)
        g.tensor.wait_ge(sem["arr%d" % slot], 2 * _count(topo.mask(s, core)))
        for b in slices:
            mm = g.tensor.matmul_mx(bank(b), T.s_q[:, cols(b, NC)], T.s_s[:, cols(b, NC)],
                                    T.l_q[:, cols(slot, NC)], T.l_s[:, cols(slot, NC)], False, j == len(due) - 1)
            if j == len(due) - 1:
                mm.then_inc(sem["y_%d" % b], 1)

    for n, b in enumerate(slices):
        if n % 2 == 0:
            g.scalar.wait_ge(sem["y_%d" % b], 1)
            g.scalar.activation(T.y_t[:, b:TW:4], bank(b), ActivationFunctionType.Copy).then_inc(sem.copied, 1)
        else:
            g.vector.wait_ge(sem["y_%d" % b], 1)
            g.vector.tensor_copy(T.y_t[:, b:TW:4], bank(b)).then_inc(sem.copied, 1)
    g.sync.wait_ge(sem.copied, 4)
    g.sync.dma_start(T.y[:], T.y_t[:]).then_inc(sem.stored, 16)
    g.sync.wait_ge(sem.stored, 16)
    g.wait_ge(sem.sent, sent)
